import numpy as np
import ml_dtypes


def mxq(x, axis, fmt="e4m3"):
    dtype, down = {"e4m3": (ml_dtypes.float8_e4m3fn, 7), "e5m2": (ml_dtypes.float8_e5m2, 14)}[fmt]
    v = np.moveaxis(np.asarray(x, np.float32).astype(ml_dtypes.bfloat16).astype(np.float64), axis, -1)
    blocks = v.reshape(v.shape[:-1] + (-1, 32))
    amax = np.abs(blocks).max(-1, keepdims=True)
    byte = np.maximum(np.where(amax > 0, np.frexp(amax)[1] - 1 + 127, 0) - down, 1)
    scale = np.exp2(byte - 127.0)
    codes = (blocks / scale).astype(np.float32).astype(dtype).astype(np.float64)
    return np.moveaxis((codes * scale).reshape(v.shape), -1, axis)


WIDE = False


def mx_kscale(k):
    if not WIDE:
        return np.ones(k)
    levels = np.array([10, -10, 5, -5, 0])
    if k % 512:
        return np.exp2(np.random.permutation(np.resize(levels, k // 32))).repeat(32)
    a = np.empty((k // 512, 16))
    for p in range(k // 512):
        a[p, :8] = np.random.permutation(np.resize(levels, 8))
        for g in range(8):
            far = levels[np.abs(levels - a[p, g]) >= 10]
            a[p, g + 8] = far[np.random.randint(len(far))]
    return np.exp2(a.ravel()).repeat(32)


BF16 = ml_dtypes.bfloat16


def bf(x):
    return np.asarray(x, np.float32).astype(BF16)


def f64(x):
    return np.asarray(x).astype(np.float64)


E2M1 = np.array([0.0, 0.5, 1.0, 1.5, 2.0, 3.0, 4.0, 6.0, -0.0, -0.5, -1.0, -1.5, -2.0, -3.0, -4.0, -6.0])


def pack_weight(w, fmt):
    k, n = w.shape
    w = f64(bf(w)).reshape(k // 32, 32, n)
    amax = np.abs(w).max(1)
    if fmt == "e4m3":
        byte = np.frexp(amax)[1] - 1 + 127 - 7
    else:
        mant, ex = np.frexp(amax / 6.0)
        byte = np.where(mant > 0.5, ex, ex - 1) + 127
    byte = np.clip(np.where(amax > 0, byte, 1), 1, 254)
    scaled = (w * np.exp2(127.0 - byte)[:, None, :]).reshape(k, n).astype(np.float32)
    by_word = np.ascontiguousarray(scaled.reshape(k // 512, 128, 4, n).transpose(0, 1, 3, 2))
    if fmt == "e4m3":
        words = by_word.astype(ml_dtypes.float8_e4m3fn).view(np.uint8)
    else:
        c = by_word.astype(ml_dtypes.float4_e2m1fn).view(np.uint8) & 0xF
        words = c[..., 0::2] | (c[..., 1::2] << 4)
    return np.ascontiguousarray(words), np.ascontiguousarray(byte.astype(np.uint8).reshape(k // 512, 16, n))


def unpack_weight(words, scales, fmt):
    g, p, n, _ = words.shape
    if fmt == "e4m3":
        vals = np.ascontiguousarray(words).view(ml_dtypes.float8_e4m3fn).astype(np.float64)
    else:
        nib = np.empty((g, p, n, 4), np.uint8)
        nib[..., 0::2] = words & 0xF
        nib[..., 1::2] = words >> 4
        vals = E2M1[nib]
    vals = vals * np.repeat(np.exp2(scales.astype(np.float64) - 127.0), 8, axis=1)[..., None]
    return vals.transpose(0, 1, 3, 2).reshape(g * 512, n)
def pack4(w):
    words, scales = pack_weight(w, "e2m1")
    return words.reshape(words.shape[0], 128, -1), scales


def unpack4(words, scales):
    return unpack_weight(words.reshape(words.shape[0], 128, -1, 2), scales, "e2m1")


M, K, N = 1024, 1024, 1536


def setup_inputs():
    s = mx_kscale(K)
    u = np.random.standard_normal((M, K)) * s
    v = np.random.standard_normal((K, N)) / np.sqrt(K) / s[:, None]
    c = np.random.standard_normal((K, N)) / np.sqrt(K) / s[:, None]
    d = np.random.standard_normal((K, N)) / np.sqrt(K) / s[:, None]
    mask = np.random.random_sample((M, N)) < 0.5
    y = np.random.standard_normal((M, N)) * mask
    v_words, v_scales = pack4(v)
    c_words, c_scales = pack_weight(c, "e4m3")
    return {"u": bf(u),
            "v_words": v_words, "v_scales": v_scales,
            "c_words": c_words, "c_scales": c_scales,
            "d": bf(d),
            "y": bf(y)}


def reference(u, v_words, v_scales, c_words, c_scales, d, y):
    uq = mxq(f64(u), 1, "e4m3")
    pred = uq @ unpack4(v_words, v_scales)
    conf = uq @ unpack_weight(c_words, c_scales, "e4m3")
    step = uq @ mxq(f64(d), 0, "e4m3")
    weight = 1.0 / (1.0 + np.exp(-conf))
    residual = weight * (pred - f64(y))
    slope = residual * step
    return residual, slope

@@ -1,0 +1,272 @@
+from contextlib import ExitStack
+
+import concourse.mybir as mybir
+from concourse.masks import make_identity
+
+M, K, N = 1024, 1024, 1536
+FLOPS = 3 * 2 * M * K * N
+
+F32 = mybir.dt.float32
+BF16 = mybir.dt.bfloat16
+I32 = mybir.dt.int32
+U32 = mybir.dt.uint32
+U8 = mybir.dt.uint8
+FP8X4 = mybir.dt.float8_e4m3fn_x4
+FP4X4 = mybir.dt.float4_e2m1fn_x4
+ALU = mybir.AluOpType
+SIGMOID = mybir.ActivationFunctionType.Sigmoid
+
+P = 128
+PACK = 4
+PASSES = K // (P * PACK)
+ROW_TILES = M // P
+N_TILE = 512
+COL_TILES = N // N_TILE
+BANKS = 8
+
+
+def tile_sensing_residual_slope_s10_kernel(
+    tc, u, v_words, v_scales, c_words, c_scales, d, y, out_0, out_1
+):
+    nc = tc.nc
+    u_rows = u.rearrange("(p j) k -> p j k", j=ROW_TILES)
+    y_rows = y.rearrange("(p j) n -> p j n", j=ROW_TILES)
+    residual_rows = out_0.rearrange("(p j) n -> p j n", j=ROW_TILES)
+    slope_rows = out_1.rearrange("(p j) n -> p j n", j=ROW_TILES)
+
+    with ExitStack() as ctx:
+        keep = ctx.enter_context(tc.tile_pool(name="keep", bufs=1))
+        stage = ctx.enter_context(tc.tile_pool(name="stage", bufs=2))
+        psum = ctx.enter_context(tc.psum_pool(name="psum", bufs=1))
+        ctx.enter_context(tc.manual_schedule())
+
+        banks_taken = []
+
+        def next_bank():
+            name = "bank%d" % (len(banks_taken) % BANKS)
+            banks_taken.append(name)
+            return psum.tile([P, N_TILE], F32, name=name, tag=name)
+
+        def cols(n):
+            return slice(n * N_TILE, (n + 1) * N_TILE)
+
+        planes = keep.tile([P, PASSES * N], U8, align_bytes=64)
+        nc.vector.memset(planes[:].bitcast(I32), 0)
+        identity = keep.tile([P, P], F32)
+        make_identity(nc, identity[:])
+
+        u_raw, y_raw, c_codes, d_raw = {}, {}, {}, {}
+
+        def load_rows(store, hbm, name, first, count):
+            width = hbm.shape[2]
+            raw = keep.tile([P, count * width], BF16, name="%s%d" % (name, first), align_bytes=64)
+            nc.sync.dma_start(
+                out=raw[:].rearrange("p (j w) -> p j w", j=count), in_=hbm[:, first : first + count, :]
+            )
+            for j in range(count):
+                store[first + j] = raw[:, j * width : (j + 1) * width]
+
+        def load_c(n):
+            codes = keep.tile([P, PASSES * N_TILE], U32, name="c_codes%d" % n, align_bytes=64)
+            hbm = c_words.rearrange("g p n t -> p g (n t)")[:, :, n * N_TILE * PACK : (n + 1) * N_TILE * PACK]
+            nc.sync.dma_start(
+                out=codes[:].bitcast(I32).rearrange("p (g n) -> p g n", g=PASSES), in_=hbm.bitcast(I32)
+            )
+            c_codes[n] = codes
+
+        def load_d(g):
+            raw = keep.tile([P, PACK, N], BF16, name="d_raw%d" % g, align_bytes=64)
+            nc.sync.dma_start(out=raw[:], in_=d.rearrange("(g p t) n -> g p t n", g=PASSES, t=PACK)[g])
+            d_raw[g] = raw
+
+        load_rows(u_raw, u_rows, "u_raw", 0, 1)
+        load_rows(u_raw, u_rows, "u_raw", 1, 1)
+        for q in range(4):
+            nc.sync.dma_start(
+                out=planes[32 * q : 32 * q + 4, :].bitcast(I32).rearrange("r (g x) -> r g x", g=PASSES),
+                in_=v_scales[:, 4 * q : 4 * q + 4, :].rearrange("g r n -> r g n").bitcast(I32),
+            )
+        v_codes = keep.tile([P, PASSES * 2 * N], U8, align_bytes=64)
+        nc.sync.dma_start(
+            out=v_codes[:].bitcast(I32).rearrange("p (g x) -> p g x", g=PASSES),
+            in_=v_words.rearrange("g p x -> p g x").bitcast(I32),
+        )
+        warm = keep.tile([P, 1], F32)
+        nc.scalar.activation(out=warm[:], in_=identity[:, 0:1], func=SIGMOID)
+        for q in range(4):
+            nc.sync.dma_start(
+                out=planes[32 * q + 4 : 32 * q + 12, 0:N].bitcast(I32),
+                in_=c_scales[:, 4 * q : 4 * q + 4, :].bitcast(I32),
+            )
+        load_c(0)
+        load_rows(y_raw, y_rows, "y_raw", 0, 1)
+        load_c(1)
+        load_rows(y_raw, y_rows, "y_raw", 1, 1)
+        load_rows(u_raw, u_rows, "u_raw", 2, 2)
+        load_c(2)
+        load_rows(y_raw, y_rows, "y_raw", 2, 1)
+        load_d(0)
+        load_rows(u_raw, u_rows, "u_raw", 4, 2)
+        load_rows(y_raw, y_rows, "y_raw", 3, 1)
+        load_d(1)
+        load_rows(y_raw, y_rows, "y_raw", 4, 2)
+        load_rows(u_raw, u_rows, "u_raw", 6, 2)
+        load_rows(y_raw, y_rows, "y_raw", 6, 2)
+
+        u_codes = keep.tile([P, ROW_TILES * PASSES * P], U32, align_bytes=64)
+        u_scales = keep.tile([P, ROW_TILES * PASSES * P], U8, align_bytes=64)
+        d_codes = keep.tile([P, COL_TILES * PASSES * N_TILE], U32, align_bytes=64)
+        d_scales = keep.tile([P, COL_TILES * PASSES * N_TILE], U8, align_bytes=64)
+
+        def turn_u(first, count):
+            grouped = stage.tile([P, count * K], BF16, name="u_grouped", tag="u_grouped", align_bytes=64)
+            turned = []
+            for j in range(first, first + count):
+                words = u_raw[j].bitcast(F32)
+                bank = next_bank()
+                for g in range(PASSES):
+                    for h in range(2):
+                        at = (2 * g + h) * P
+                        nc.tensor.transpose(
+                            bank[:, at : at + P], words[:, 2 * P * g + h : 2 * P * (g + 1) : 2], identity[:]
+                        )
+                turned.append(bank)
+            for i in range(count):
+                dst = grouped[:, i * K : (i + 1) * K].bitcast(F32).rearrange("p (g r h) -> p g r h", g=PASSES, h=2)
+                src = turned[i][:].rearrange("p (g h r) -> p g r h", g=PASSES, h=2)
+                if (first + i) % 2 == 0:
+                    nc.vector.tensor_copy(out=dst, in_=src)
+                else:
+                    nc.scalar.copy(out=dst, in_=src)
+            return grouped
+
+        def quantize_u(grouped, first, count):
+            at = slice(first * PASSES * P, (first + count) * PASSES * P)
+            nc.vector.quantize_mx(out=u_codes[:, at].bitcast(FP8X4), scales=u_scales[:, at], in_=grouped[:])
+
+        d_grouped = {}
+
+        def interleave_d(g, n, copy, part, parts):
+            if (g, n) not in d_grouped:
+                d_grouped[(g, n)] = stage.tile(
+                    [P, N_TILE * PACK], BF16, name="d_grouped", tag="d_grouped", bufs=3, align_bytes=64
+                )
+            width = N_TILE // parts
+            dst = d_grouped[(g, n)][:, part * width * PACK : (part + 1) * width * PACK]
+            src = d_raw[g][:, :, n * N_TILE + part * width : n * N_TILE + (part + 1) * width]
+            copy(
+                out=dst.rearrange("p (c i t) -> p c t i", i=4, t=PACK),
+                in_=src.rearrange("p t (c i) -> p c t i", i=4),
+            )
+
+        def quantize_d(g, n):
+            at = slice((n * PASSES + g) * N_TILE, (n * PASSES + g + 1) * N_TILE)
+            nc.vector.quantize_mx(
+                out=d_codes[:, at].bitcast(FP8X4), scales=d_scales[:, at], in_=d_grouped[(g, n)][:]
+            )
+
+        def product(j, rhs, rhs_scale):
+            bank = next_bank()
+            for g in range(PASSES):
+                at = slice((j * PASSES + g) * P, (j * PASSES + g + 1) * P)
+                nc.tensor.matmul_mx(
+                    out=bank[:],
+                    lhsT=u_codes[:, at].bitcast(FP8X4),
+                    lhsT_scale=u_scales[:, at],
+                    rhs=rhs(g),
+                    rhs_scale=rhs_scale(g),
+                    start=(g == 0),
+                    stop=(g == PASSES - 1),
+                )
+            return bank
+
+        residual, slope = {}, {}
+
+        def residual_tile(j, n):
+            if n == 0:
+                residual[j] = keep.tile([P, N], F32, name="residual%d" % j)
+            pred = product(
+                j,
+                lambda g: v_codes[:, 2 * (g * N + n * N_TILE) : 2 * (g * N + (n + 1) * N_TILE)].bitcast(FP4X4),
+                lambda g: planes[:, g * N + n * N_TILE : g * N + (n + 1) * N_TILE],
+            )
+            conf = product(
+                j,
+                lambda g: c_codes[n][:, cols(g)].bitcast(FP8X4),
+                lambda g: planes[4 + 4 * g : P, cols(n)],
+            )
+            nc.vector.tensor_tensor(
+                out=residual[j][:, cols(n)], in0=pred[:], in1=y_raw[j][:, cols(n)], op=ALU.subtract
+            )
+            weight = stage.tile([P, N_TILE], F32, name="weight", tag="weight", bufs=6)
+            nc.scalar.activation(out=weight[:], in_=conf[:], func=SIGMOID)
+            nc.gpsimd.tensor_tensor(
+                out=residual[j][:, cols(n)], in0=residual[j][:, cols(n)], in1=weight[:], op=ALU.mult
+            )
+            last_row = j == ROW_TILES - 1
+            if last_row and n == COL_TILES - 2:
+                nc.sync.dma_start(out=residual_rows[:, j, : 2 * N_TILE], in_=residual[j][:, : 2 * N_TILE])
+            elif last_row and n == COL_TILES - 1:
+                nc.sync.dma_start(out=residual_rows[:, j, cols(n)], in_=residual[j][:, cols(n)])
+            elif n == COL_TILES - 1:
+                nc.sync.dma_start(out=residual_rows[:, j, :], in_=residual[j][:])
+
+        EARLY_ROWS = 5
+
+        def slope_tile(j, n):
+            if n == 0:
+                slope[j] = stage.tile([P, N], F32, name="slope", tag="slope", bufs=6)
+            at = n * PASSES
+            step = product(
+                j,
+                lambda g: d_codes[:, cols(at + g)].bitcast(FP8X4),
+                lambda g: d_scales[:, cols(at + g)],
+            )
+            nc.vector.tensor_tensor(
+                out=slope[j][:, cols(n)], in0=step[:], in1=residual[j][:, cols(n)], op=ALU.mult
+            )
+            if j == ROW_TILES - 1 or (j < EARLY_ROWS and n == COL_TILES - 1):
+                nc.sync.dma_start(out=slope_rows[:, j, cols(n)], in_=slope[j][:, cols(n)])
+            elif j < EARLY_ROWS and n == COL_TILES - 2:
+                nc.sync.dma_start(out=slope_rows[:, j, : 2 * N_TILE], in_=slope[j][:, : 2 * N_TILE])
+            elif n == COL_TILES - 1:
+                nc.sync.dma_start(out=slope_rows[:, j, :], in_=slope[j][:])
+
+        first_order = [(j, n) for n in range(COL_TILES) for j in range(2)]
+        first_order.extend([(j, n) for j in range(2, ROW_TILES) for n in range(COL_TILES)])
+        second_order = [(j, n) for n in range(COL_TILES) for j in range(EARLY_ROWS)]
+        second_order.extend([(j, n) for j in range(EARLY_ROWS, ROW_TILES) for n in range(COL_TILES)])
+
+        grouped0 = turn_u(0, 1)
+        grouped1 = turn_u(1, 1)
+        quantize_u(grouped0, 0, 1)
+        quantize_u(grouped1, 1, 1)
+
+        turn_after = {3: 2, 9: 4, 15: 6}
+        scalar_parts = {
+            7: [(0, 0, 0)], 8: [(0, 0, 1)], 10: [(0, 1, 0)], 11: [(0, 1, 1)],
+            12: [(1, 1, 0)], 13: [(1, 1, 1)], 14: [(0, 2, 0), (0, 2, 1)], 15: [(1, 2, 0), (1, 2, 1)],
+        }
+        quantize_after = {9: [(0, 0)], 12: [(0, 1)], 13: [(1, 0)], 14: [(1, 1)], 15: [(0, 2)], 16: [(1, 2)]}
+        waiting = None
+        done = 0
+        for i, (j, n) in enumerate(first_order):
+            residual_tile(j, n)
+            if waiting is not None:
+                quantize_u(waiting[0], waiting[1], 2)
+                waiting = None
+            for g, c in quantize_after.get(i, []):
+                quantize_d(g, c)
+            if i == 12:
+                interleave_d(1, 0, nc.vector.tensor_copy, 0, 1)
+            for g, c, part in scalar_parts.get(i, []):
+                interleave_d(g, c, nc.scalar.copy, part, 2)
+            if i in turn_after:
+                waiting = (turn_u(turn_after[i], 2), turn_after[i])
+            if i >= 14:
+                for extra in range(3):
+                    if first_order.index(second_order[done]) <= i - 2:
+                        slope_tile(*second_order[done])
+                        done = done + 1
+        for j, n in second_order[done:]:
+            slope_tile(j, n)

@@ -23,6 +23,17 @@ ROW_TILES = M // P
 N_TILE = 512
 COL_TILES = N // N_TILE
 BANKS = 8
+QUADRANT = 32
+SCALE_ROWS = 4
+QUADRANT_ORDER = (0, 2, 1, 3)
+
+FIRST_GPSIMD_ROW = 4
+SCALAR_TURNED_ROWS = (1, 2, 3)
+TURN_AHEAD = 4
+FIRST_D_STEP = 5
+D_PAUSE_STEP = 9
+SLOPES_PER_STEP = 3
+ROWS_BY_COLUMN = 6
 
 
 def tile_sensing_residual_slope_s10_kernel(
@@ -33,6 +44,9 @@ def tile_sensing_residual_slope_s10_kernel(
     y_rows = y.rearrange("(p j) n -> p j n", j=ROW_TILES)
     residual_rows = out_0.rearrange("(p j) n -> p j n", j=ROW_TILES)
     slope_rows = out_1.rearrange("(p j) n -> p j n", j=ROW_TILES)
+    v_bytes = v_words.rearrange("g p x -> p g x")
+    c_bytes = c_words.rearrange("g p n t -> p g (n t)")
+    d_passes = d.rearrange("(g p t) n -> g p t n", g=PASSES, t=PACK)
 
     with ExitStack() as ctx:
         keep = ctx.enter_context(tc.tile_pool(name="keep", bufs=1))
@@ -50,122 +64,135 @@ def tile_sensing_residual_slope_s10_kernel(
         def cols(n):
             return slice(n * N_TILE, (n + 1) * N_TILE)
 
-        planes = keep.tile([P, PASSES * N], U8, align_bytes=64)
-        nc.vector.memset(planes[:].bitcast(I32), 0)
+        v_scale_tile = keep.tile([P, PASSES * N], U8, align_bytes=64)
+        nc.vector.memset(v_scale_tile[:].bitcast(I32), 0)
+        c_scale_tile = keep.tile([P, N], U8, align_bytes=64)
+        nc.vector.memset(c_scale_tile[:].bitcast(I32), 0)
         identity = keep.tile([P, P], F32)
         make_identity(nc, identity[:])
 
-        u_raw, y_raw, c_codes, d_raw = {}, {}, {}, {}
+        u_raw, y_raw, v_codes, c_codes, d_raw = {}, {}, {}, {}, {}
 
-        def load_rows(store, hbm, name, first, count):
+        def load_rows(loaded, hbm, name, first, count):
             width = hbm.shape[2]
             raw = keep.tile([P, count * width], BF16, name="%s%d" % (name, first), align_bytes=64)
             nc.sync.dma_start(
                 out=raw[:].rearrange("p (j w) -> p j w", j=count), in_=hbm[:, first : first + count, :]
             )
             for j in range(count):
-                store[first + j] = raw[:, j * width : (j + 1) * width]
+                loaded[first + j] = raw[:, j * width : (j + 1) * width]
 
-        def load_c(n):
-            codes = keep.tile([P, PASSES * N_TILE], U32, name="c_codes%d" % n, align_bytes=64)
-            hbm = c_words.rearrange("g p n t -> p g (n t)")[:, :, n * N_TILE * PACK : (n + 1) * N_TILE * PACK]
+        def load_u(first, count):
+            load_rows(u_raw, u_rows, "u_raw", first, count)
+
+        def load_y(first, count):
+            load_rows(y_raw, y_rows, "y_raw", first, count)
+
+        def load_words(loaded, hbm, name, word_bytes, first, count):
+            width = N_TILE * word_bytes
+            raw = keep.tile([P, PASSES * count * width], U8, name="%s%d" % (name, first), align_bytes=64)
             nc.sync.dma_start(
-                out=codes[:].bitcast(I32).rearrange("p (g n) -> p g n", g=PASSES), in_=hbm.bitcast(I32)
+                out=raw[:].bitcast(I32).rearrange("p (g x) -> p g x", g=PASSES),
+                in_=hbm[:, :, first * width : (first + count) * width].bitcast(I32),
             )
-            c_codes[n] = codes
+            for g in range(PASSES):
+                for n in range(count):
+                    at = (g * count + n) * width
+                    loaded[(g, first + n)] = raw[:, at : at + width]
+
+        def load_v(first, count):
+            load_words(v_codes, v_bytes, "v_codes", 2, first, count)
+
+        def load_c(first, count):
+            load_words(c_codes, c_bytes, "c_codes", 4, first, count)
 
         def load_d(g):
             raw = keep.tile([P, PACK, N], BF16, name="d_raw%d" % g, align_bytes=64)
-            nc.sync.dma_start(out=raw[:], in_=d.rearrange("(g p t) n -> g p t n", g=PASSES, t=PACK)[g])
+            nc.sync.dma_start(out=raw[:], in_=d_passes[g])
             d_raw[g] = raw
 
-        load_rows(u_raw, u_rows, "u_raw", 0, 1)
-        load_rows(u_raw, u_rows, "u_raw", 1, 1)
-        for q in range(4):
+        load_u(0, 1)
+        for q in QUADRANT_ORDER:
+            rows = v_scale_tile[QUADRANT * q : QUADRANT * q + SCALE_ROWS, :]
             nc.sync.dma_start(
-                out=planes[32 * q : 32 * q + 4, :].bitcast(I32).rearrange("r (g x) -> r g x", g=PASSES),
-                in_=v_scales[:, 4 * q : 4 * q + 4, :].rearrange("g r n -> r g n").bitcast(I32),
+                out=rows.bitcast(I32).rearrange("r (g x) -> r g x", g=PASSES),
+                in_=v_scales[:, SCALE_ROWS * q : SCALE_ROWS * (q + 1), :].rearrange("g r n -> r g n").bitcast(I32),
             )
-        v_codes = keep.tile([P, PASSES * 2 * N], U8, align_bytes=64)
-        nc.sync.dma_start(
-            out=v_codes[:].bitcast(I32).rearrange("p (g x) -> p g x", g=PASSES),
-            in_=v_words.rearrange("g p x -> p g x").bitcast(I32),
-        )
-        warm = keep.tile([P, 1], F32)
-        nc.scalar.activation(out=warm[:], in_=identity[:, 0:1], func=SIGMOID)
-        for q in range(4):
+        load_v(0, 1)
+        for q in QUADRANT_ORDER:
+            rows = c_scale_tile[QUADRANT * q + SCALE_ROWS : QUADRANT * q + (PASSES + 1) * SCALE_ROWS, :]
             nc.sync.dma_start(
-                out=planes[32 * q + 4 : 32 * q + 12, 0:N].bitcast(I32),
-                in_=c_scales[:, 4 * q : 4 * q + 4, :].bitcast(I32),
+                out=rows.bitcast(I32), in_=c_scales[:, SCALE_ROWS * q : SCALE_ROWS * (q + 1), :].bitcast(I32)
             )
-        load_c(0)
-        load_rows(y_raw, y_rows, "y_raw", 0, 1)
-        load_c(1)
-        load_rows(y_raw, y_rows, "y_raw", 1, 1)
-        load_rows(u_raw, u_rows, "u_raw", 2, 2)
-        load_c(2)
-        load_rows(y_raw, y_rows, "y_raw", 2, 1)
+        load_c(0, 1)
+        load_u(1, 1)
+        load_v(1, 2)
+        load_c(1, 1)
+        load_y(0, 1)
+        load_u(2, 2)
+        load_y(1, 1)
+        load_c(2, 1)
         load_d(0)
-        load_rows(u_raw, u_rows, "u_raw", 4, 2)
-        load_rows(y_raw, y_rows, "y_raw", 3, 1)
+        load_y(2, 1)
+        load_u(4, 2)
+        load_y(3, 1)
         load_d(1)
-        load_rows(y_raw, y_rows, "y_raw", 4, 2)
-        load_rows(u_raw, u_rows, "u_raw", 6, 2)
-        load_rows(y_raw, y_rows, "y_raw", 6, 2)
+        load_y(4, 2)
+        load_u(6, 2)
+        load_y(6, 2)
 
         u_codes = keep.tile([P, ROW_TILES * PASSES * P], U32, align_bytes=64)
         u_scales = keep.tile([P, ROW_TILES * PASSES * P], U8, align_bytes=64)
         d_codes = keep.tile([P, COL_TILES * PASSES * N_TILE], U32, align_bytes=64)
         d_scales = keep.tile([P, COL_TILES * PASSES * N_TILE], U8, align_bytes=64)
+        u_grouped, d_grouped = {}, {}
 
         def turn_u(first, count):
             grouped = stage.tile([P, count * K], BF16, name="u_grouped", tag="u_grouped", align_bytes=64)
+            u_grouped[first] = grouped
             turned = []
             for j in range(first, first + count):
-                words = u_raw[j].bitcast(F32)
+                pairs = u_raw[j].bitcast(F32)
                 bank = next_bank()
                 for g in range(PASSES):
                     for h in range(2):
                         at = (2 * g + h) * P
                         nc.tensor.transpose(
-                            bank[:, at : at + P], words[:, 2 * P * g + h : 2 * P * (g + 1) : 2], identity[:]
+                            bank[:, at : at + P], pairs[:, 2 * P * g + h : 2 * P * (g + 1) : 2], identity[:]
                         )
                 turned.append(bank)
             for i in range(count):
-                dst = grouped[:, i * K : (i + 1) * K].bitcast(F32).rearrange("p (g r h) -> p g r h", g=PASSES, h=2)
-                src = turned[i][:].rearrange("p (g h r) -> p g r h", g=PASSES, h=2)
-                if (first + i) % 2 == 0:
-                    nc.vector.tensor_copy(out=dst, in_=src)
-                else:
-                    nc.scalar.copy(out=dst, in_=src)
-            return grouped
-
-        def quantize_u(grouped, first, count):
-            at = slice(first * PASSES * P, (first + count) * PASSES * P)
-            nc.vector.quantize_mx(out=u_codes[:, at].bitcast(FP8X4), scales=u_scales[:, at], in_=grouped[:])
-
-        d_grouped = {}
-
-        def interleave_d(g, n, copy, part, parts):
-            if (g, n) not in d_grouped:
-                d_grouped[(g, n)] = stage.tile(
-                    [P, N_TILE * PACK], BF16, name="d_grouped", tag="d_grouped", bufs=3, align_bytes=64
+                copy = nc.scalar.copy if first + i in SCALAR_TURNED_ROWS else nc.vector.tensor_copy
+                side_by_side = grouped[:, i * K : (i + 1) * K].bitcast(F32)
+                copy(
+                    out=side_by_side.rearrange("p (g r h) -> p g r h", g=PASSES, h=2),
+                    in_=turned[i][:].rearrange("p (g h r) -> p g r h", g=PASSES, h=2),
                 )
-            width = N_TILE // parts
-            dst = d_grouped[(g, n)][:, part * width * PACK : (part + 1) * width * PACK]
-            src = d_raw[g][:, :, n * N_TILE + part * width : n * N_TILE + (part + 1) * width]
-            copy(
-                out=dst.rearrange("p (c i t) -> p c t i", i=4, t=PACK),
-                in_=src.rearrange("p t (c i) -> p c t i", i=4),
-            )
 
-        def quantize_d(g, n):
-            at = slice((n * PASSES + g) * N_TILE, (n * PASSES + g + 1) * N_TILE)
+        def quantize_u(first, count):
+            at = slice(first * PASSES * P, (first + count) * PASSES * P)
             nc.vector.quantize_mx(
-                out=d_codes[:, at].bitcast(FP8X4), scales=d_scales[:, at], in_=d_grouped[(g, n)][:]
+                out=u_codes[:, at].bitcast(FP8X4), scales=u_scales[:, at], in_=u_grouped[first][:]
             )
 
-        def product(j, rhs, rhs_scale):
+        def interleave_d(g, n, half):
+            if n not in d_grouped:
+                d_grouped[n] = stage.tile(
+                    [P, PASSES * N_TILE * PACK], BF16, name="d_grouped", tag="d_grouped", align_bytes=64
+                )
+            width = N_TILE // 2
+            at = (g * N_TILE + half * width) * PACK
+            first = n * N_TILE + half * width
+            nc.scalar.copy(
+                out=d_grouped[n][:, at : at + width * PACK].rearrange("p (c i t) -> p c t i", i=4, t=PACK),
+                in_=d_raw[g][:, :, first : first + width].rearrange("p t (c i) -> p c t i", i=4),
+            )
+
+        def quantize_d(n):
+            at = slice(n * PASSES * N_TILE, (n + 1) * PASSES * N_TILE)
+            nc.vector.quantize_mx(out=d_codes[:, at].bitcast(FP8X4), scales=d_scales[:, at], in_=d_grouped[n][:])
+
+        def product(j, moving, moving_scales):
             bank = next_bank()
             for g in range(PASSES):
                 at = slice((j * PASSES + g) * P, (j * PASSES + g + 1) * P)
@@ -173,100 +200,106 @@ def tile_sensing_residual_slope_s10_kernel(
                     out=bank[:],
                     lhsT=u_codes[:, at].bitcast(FP8X4),
                     lhsT_scale=u_scales[:, at],
-                    rhs=rhs(g),
-                    rhs_scale=rhs_scale(g),
+                    rhs=moving[g],
+                    rhs_scale=moving_scales[g],
                     start=(g == 0),
                     stop=(g == PASSES - 1),
                 )
             return bank
 
-        residual, slope = {}, {}
+        residual, pred, weight = {}, {}, {}
 
-        def residual_tile(j, n):
-            if n == 0:
-                residual[j] = keep.tile([P, N], F32, name="residual%d" % j)
-            pred = product(
+        def predict(j, n):
+            pred[(j, n)] = product(
                 j,
-                lambda g: v_codes[:, 2 * (g * N + n * N_TILE) : 2 * (g * N + (n + 1) * N_TILE)].bitcast(FP4X4),
-                lambda g: planes[:, g * N + n * N_TILE : g * N + (n + 1) * N_TILE],
+                [v_codes[(g, n)].bitcast(FP4X4) for g in range(PASSES)],
+                [v_scale_tile[:, cols(g * COL_TILES + n)] for g in range(PASSES)],
             )
             conf = product(
                 j,
-                lambda g: c_codes[n][:, cols(g)].bitcast(FP8X4),
-                lambda g: planes[4 + 4 * g : P, cols(n)],
+                [c_codes[(g, n)].bitcast(FP8X4) for g in range(PASSES)],
+                [c_scale_tile[SCALE_ROWS * (g + 1) : P, cols(n)] for g in range(PASSES)],
             )
+            weight[(j, n)] = stage.tile([P, N_TILE], F32, name="weight", tag="weight", bufs=8)
+            nc.scalar.activation(out=weight[(j, n)][:], in_=conf[:], func=SIGMOID)
+
+        def subtract(j, n):
+            if n == 0:
+                residual[j] = keep.tile([P, N], F32, name="residual%d" % j)
             nc.vector.tensor_tensor(
-                out=residual[j][:, cols(n)], in0=pred[:], in1=y_raw[j][:, cols(n)], op=ALU.subtract
+                out=residual[j][:, cols(n)], in0=pred[(j, n)][:], in1=y_raw[j][:, cols(n)], op=ALU.subtract
             )
-            weight = stage.tile([P, N_TILE], F32, name="weight", tag="weight", bufs=6)
-            nc.scalar.activation(out=weight[:], in_=conf[:], func=SIGMOID)
-            nc.gpsimd.tensor_tensor(
-                out=residual[j][:, cols(n)], in0=residual[j][:, cols(n)], in1=weight[:], op=ALU.mult
-            )
-            last_row = j == ROW_TILES - 1
-            if last_row and n == COL_TILES - 2:
-                nc.sync.dma_start(out=residual_rows[:, j, : 2 * N_TILE], in_=residual[j][:, : 2 * N_TILE])
-            elif last_row and n == COL_TILES - 1:
+
+        def weigh(engine, j, n):
+            part = residual[j][:, cols(n)]
+            engine.tensor_tensor(out=part, in0=part, in1=weight[(j, n)][:], op=ALU.mult)
+
+        def store_residual(j, n):
+            if j == ROW_TILES - 1:
                 nc.sync.dma_start(out=residual_rows[:, j, cols(n)], in_=residual[j][:, cols(n)])
             elif n == COL_TILES - 1:
                 nc.sync.dma_start(out=residual_rows[:, j, :], in_=residual[j][:])
 
-        EARLY_ROWS = 5
+        def on_gpsimd(j, n):
+            return j >= FIRST_GPSIMD_ROW and (j, n) != (ROW_TILES - 1, COL_TILES - 1)
+
+        def finish(j, n):
+            if not on_gpsimd(j, n):
+                weigh(nc.vector, j, n)
+            store_residual(j, n)
 
         def slope_tile(j, n):
-            if n == 0:
-                slope[j] = stage.tile([P, N], F32, name="slope", tag="slope", bufs=6)
-            at = n * PASSES
             step = product(
                 j,
-                lambda g: d_codes[:, cols(at + g)].bitcast(FP8X4),
-                lambda g: d_scales[:, cols(at + g)],
+                [d_codes[:, cols(n * PASSES + g)].bitcast(FP8X4) for g in range(PASSES)],
+                [d_scales[:, cols(n * PASSES + g)] for g in range(PASSES)],
             )
-            nc.vector.tensor_tensor(
-                out=slope[j][:, cols(n)], in0=step[:], in1=residual[j][:, cols(n)], op=ALU.mult
-            )
-            if j == ROW_TILES - 1 or (j < EARLY_ROWS and n == COL_TILES - 1):
-                nc.sync.dma_start(out=slope_rows[:, j, cols(n)], in_=slope[j][:, cols(n)])
-            elif j < EARLY_ROWS and n == COL_TILES - 2:
-                nc.sync.dma_start(out=slope_rows[:, j, : 2 * N_TILE], in_=slope[j][:, : 2 * N_TILE])
-            elif n == COL_TILES - 1:
-                nc.sync.dma_start(out=slope_rows[:, j, :], in_=slope[j][:])
+            slope = stage.tile([P, N_TILE], F32, name="slope", tag="slope", bufs=16)
+            nc.vector.tensor_tensor(out=slope[:], in0=step[:], in1=residual[j][:, cols(n)], op=ALU.mult)
+            nc.sync.dma_start(out=slope_rows[:, j, cols(n)], in_=slope[:])
 
-        first_order = [(j, n) for n in range(COL_TILES) for j in range(2)]
-        first_order.extend([(j, n) for j in range(2, ROW_TILES) for n in range(COL_TILES)])
-        second_order = [(j, n) for n in range(COL_TILES) for j in range(EARLY_ROWS)]
-        second_order.extend([(j, n) for j in range(EARLY_ROWS, ROW_TILES) for n in range(COL_TILES)])
+        steps = [(j, n) for j in range(2) for n in range(COL_TILES - 1)]
+        steps.extend([(j, COL_TILES - 1) for j in range(2)])
+        steps.extend([(j, n) for j in range(2, ROW_TILES) for n in range(COL_TILES)])
+        slopes = [(j, n) for n in range(COL_TILES) for j in range(ROWS_BY_COLUMN)]
+        slopes.extend([(j, n) for j in range(ROWS_BY_COLUMN, ROW_TILES) for n in range(COL_TILES)])
+        halves = [(g, n, half) for g in range(PASSES) for n in range(COL_TILES - 1) for half in range(2)]
+        halves.extend([(g, COL_TILES - 1, half) for g in range(PASSES) for half in range(2)])
+        turn_after = {steps.index((j, 0)) - TURN_AHEAD: j for j in range(2, ROW_TILES, 2)}
 
-        grouped0 = turn_u(0, 1)
-        grouped1 = turn_u(1, 1)
-        quantize_u(grouped0, 0, 1)
-        quantize_u(grouped1, 1, 1)
-
-        turn_after = {3: 2, 9: 4, 15: 6}
-        scalar_parts = {
-            7: [(0, 0, 0)], 8: [(0, 0, 1)], 10: [(0, 1, 0)], 11: [(0, 1, 1)],
-            12: [(1, 1, 0)], 13: [(1, 1, 1)], 14: [(0, 2, 0), (0, 2, 1)], 15: [(1, 2, 0), (1, 2, 1)],
-        }
-        quantize_after = {9: [(0, 0)], 12: [(0, 1)], 13: [(1, 0)], 14: [(1, 1)], 15: [(0, 2)], 16: [(1, 2)]}
-        waiting = None
-        done = 0
-        for i, (j, n) in enumerate(first_order):
-            residual_tile(j, n)
-            if waiting is not None:
-                quantize_u(waiting[0], waiting[1], 2)
-                waiting = None
-            for g, c in quantize_after.get(i, []):
-                quantize_d(g, c)
-            if i == 12:
-                interleave_d(1, 0, nc.vector.tensor_copy, 0, 1)
-            for g, c, part in scalar_parts.get(i, []):
-                interleave_d(g, c, nc.scalar.copy, part, 2)
+        turn_u(0, 1)
+        quantize_u(0, 1)
+        laid_out_at = {}
+        quantized_at = {}
+        for i, (j, n) in enumerate(steps):
+            predict(j, n)
+            if i == 0:
+                turn_u(1, 1)
+                quantize_u(1, 1)
+            subtract(j, n)
+            if on_gpsimd(j, n):
+                weigh(nc.gpsimd, j, n)
+            if i > 0:
+                finish(*steps[i - 1])
+            if i - 1 in turn_after:
+                quantize_u(turn_after[i - 1], 2)
+            for ready in range(COL_TILES):
+                if laid_out_at.get(ready) == i - 2:
+                    quantize_d(ready)
+                    quantized_at[ready] = i
+            if i >= FIRST_D_STEP and i != D_PAUSE_STEP:
+                for g, column, half in halves[: 2 if quantized_at.get(0, i) < i else 1]:
+                    interleave_d(g, column, half)
+                    halves.remove((g, column, half))
+                    if (g, half) == (PASSES - 1, 1):
+                        laid_out_at[column] = i
             if i in turn_after:
-                waiting = (turn_u(turn_after[i], 2), turn_after[i])
-            if i >= 14:
-                for extra in range(3):
-                    if first_order.index(second_order[done]) <= i - 2:
-                        slope_tile(*second_order[done])
-                        done = done + 1
-        for j, n in second_order[done:]:
-            slope_tile(j, n)
+                turn_u(turn_after[i], 2)
+            for row, column in slopes[:SLOPES_PER_STEP]:
+                if steps.index((row, column)) >= i or quantized_at.get(column, i) >= i:
+                    break
+                slope_tile(row, column)
+                slopes.remove((row, column))
+        finish(*steps[-1])
+        for row, column in slopes:
+            slope_tile(row, column)

@@ -184,8 +184,8 @@ def tile_sensing_residual_slope_s10_kernel(
             at = (g * N_TILE + half * width) * PACK
             first = n * N_TILE + half * width
             nc.scalar.copy(
-                out=d_grouped[n][:, at : at + width * PACK].rearrange("p (c i t) -> p c t i", i=4, t=PACK),
-                in_=d_raw[g][:, :, first : first + width].rearrange("p t (c i) -> p c t i", i=4),
+                out=d_grouped[n][:, at : at + width * PACK].rearrange("p (c t) -> p c t", t=PACK),
+                in_=d_raw[g][:, :, first : first + width].rearrange("p t c -> p c t"),
             )
 
         def quantize_d(n):

@@ -26,12 +26,16 @@ BANKS = 8
 QUADRANT = 32
 SCALE_ROWS = 4
 QUADRANT_ORDER = (0, 2, 1, 3)
+FP4_WORD_BYTES = 2
+FP8_WORD_BYTES = 4
+PAIR = 2
 
 FIRST_GPSIMD_ROW = 4
-SCALAR_TURNED_ROWS = (1, 2, 3)
+SCALAR_TURNED_ROWS = range(1, 2 * PAIR)
 TURN_AHEAD = 4
 FIRST_D_STEP = 5
 D_PAUSE_STEP = 9
+D_QUANTIZE_LAG = 2
 SLOPES_PER_STEP = 3
 ROWS_BY_COLUMN = 6
 
@@ -64,9 +68,9 @@ def tile_sensing_residual_slope_s10_kernel(
         def cols(n):
             return slice(n * N_TILE, (n + 1) * N_TILE)
 
-        v_scale_tile = keep.tile([P, PASSES * N], U8, align_bytes=64)
+        v_scale_tile = keep.tile([P, PASSES * N], U8, align_bytes=256)
         nc.vector.memset(v_scale_tile[:].bitcast(I32), 0)
-        c_scale_tile = keep.tile([P, N], U8, align_bytes=64)
+        c_scale_tile = keep.tile([P, N], U8, align_bytes=256)
         nc.vector.memset(c_scale_tile[:].bitcast(I32), 0)
         identity = keep.tile([P, P], F32)
         make_identity(nc, identity[:])
@@ -75,12 +79,12 @@ def tile_sensing_residual_slope_s10_kernel(
 
         def load_rows(loaded, hbm, name, first, count):
             width = hbm.shape[2]
-            raw = keep.tile([P, count * width], BF16, name="%s%d" % (name, first), align_bytes=64)
+            raw = keep.tile([P, count * width], BF16, name="%s%d" % (name, first), align_bytes=256)
             nc.sync.dma_start(
                 out=raw[:].rearrange("p (j w) -> p j w", j=count), in_=hbm[:, first : first + count, :]
             )
-            for j in range(count):
-                loaded[first + j] = raw[:, j * width : (j + 1) * width]
+            for offset in range(count):
+                loaded[first + offset] = raw[:, offset * width : (offset + 1) * width]
 
         def load_u(first, count):
             load_rows(u_raw, u_rows, "u_raw", first, count)
@@ -90,83 +94,86 @@ def tile_sensing_residual_slope_s10_kernel(
 
         def load_words(loaded, hbm, name, word_bytes, first, count):
             width = N_TILE * word_bytes
-            raw = keep.tile([P, PASSES * count * width], U8, name="%s%d" % (name, first), align_bytes=64)
+            raw = keep.tile([P, PASSES * count * width], U8, name="%s%d" % (name, first), align_bytes=256)
             nc.sync.dma_start(
                 out=raw[:].bitcast(I32).rearrange("p (g x) -> p g x", g=PASSES),
                 in_=hbm[:, :, first * width : (first + count) * width].bitcast(I32),
             )
             for g in range(PASSES):
-                for n in range(count):
-                    at = (g * count + n) * width
-                    loaded[(g, first + n)] = raw[:, at : at + width]
+                for offset in range(count):
+                    at = (g * count + offset) * width
+                    loaded[(g, first + offset)] = raw[:, at : at + width]
 
         def load_v(first, count):
-            load_words(v_codes, v_bytes, "v_codes", 2, first, count)
+            load_words(v_codes, v_bytes, "v_codes", FP4_WORD_BYTES, first, count)
 
         def load_c(first, count):
-            load_words(c_codes, c_bytes, "c_codes", 4, first, count)
+            load_words(c_codes, c_bytes, "c_codes", FP8_WORD_BYTES, first, count)
 
         def load_d(g):
-            raw = keep.tile([P, PACK, N], BF16, name="d_raw%d" % g, align_bytes=64)
+            raw = keep.tile([P, PACK, N], BF16, name="d_raw%d" % g, align_bytes=256)
             nc.sync.dma_start(out=raw[:], in_=d_passes[g])
             d_raw[g] = raw
 
         load_u(0, 1)
-        for q in QUADRANT_ORDER:
-            rows = v_scale_tile[QUADRANT * q : QUADRANT * q + SCALE_ROWS, :]
+        for quadrant in QUADRANT_ORDER:
+            top = QUADRANT * quadrant
+            blocks = slice(SCALE_ROWS * quadrant, SCALE_ROWS * (quadrant + 1))
             nc.sync.dma_start(
-                out=rows.bitcast(I32).rearrange("r (g x) -> r g x", g=PASSES),
-                in_=v_scales[:, SCALE_ROWS * q : SCALE_ROWS * (q + 1), :].rearrange("g r n -> r g n").bitcast(I32),
+                out=v_scale_tile[top : top + SCALE_ROWS, :].bitcast(I32).rearrange("r (g x) -> r g x", g=PASSES),
+                in_=v_scales[:, blocks, :].rearrange("g r n -> r g n").bitcast(I32),
             )
         load_v(0, 1)
-        for q in QUADRANT_ORDER:
-            rows = c_scale_tile[QUADRANT * q + SCALE_ROWS : QUADRANT * q + (PASSES + 1) * SCALE_ROWS, :]
+        for quadrant in QUADRANT_ORDER:
+            top = QUADRANT * quadrant
+            blocks = slice(SCALE_ROWS * quadrant, SCALE_ROWS * (quadrant + 1))
             nc.sync.dma_start(
-                out=rows.bitcast(I32), in_=c_scales[:, SCALE_ROWS * q : SCALE_ROWS * (q + 1), :].bitcast(I32)
+                out=c_scale_tile[top + SCALE_ROWS : top + (PASSES + 1) * SCALE_ROWS, :].bitcast(I32),
+                in_=c_scales[:, blocks, :].bitcast(I32),
             )
         load_c(0, 1)
         load_u(1, 1)
-        load_v(1, 2)
+        load_v(1, COL_TILES - 1)
         load_c(1, 1)
         load_y(0, 1)
-        load_u(2, 2)
+        load_u(2, PAIR)
         load_y(1, 1)
         load_c(2, 1)
         load_d(0)
         load_y(2, 1)
-        load_u(4, 2)
+        load_u(4, PAIR)
         load_y(3, 1)
         load_d(1)
-        load_y(4, 2)
-        load_u(6, 2)
-        load_y(6, 2)
+        load_y(4, PAIR)
+        load_u(6, PAIR)
+        load_y(6, PAIR)
 
-        u_codes = keep.tile([P, ROW_TILES * PASSES * P], U32, align_bytes=64)
-        u_scales = keep.tile([P, ROW_TILES * PASSES * P], U8, align_bytes=64)
-        d_codes = keep.tile([P, COL_TILES * PASSES * N_TILE], U32, align_bytes=64)
-        d_scales = keep.tile([P, COL_TILES * PASSES * N_TILE], U8, align_bytes=64)
+        u_codes = keep.tile([P, ROW_TILES * PASSES * P], U32, align_bytes=256)
+        u_scales = keep.tile([P, ROW_TILES * PASSES * P], U8, align_bytes=256)
+        d_codes = keep.tile([P, COL_TILES * PASSES * N_TILE], U32, align_bytes=256)
+        d_scales = keep.tile([P, COL_TILES * PASSES * N_TILE], U8, align_bytes=256)
         u_grouped, d_grouped = {}, {}
 
         def turn_u(first, count):
-            grouped = stage.tile([P, count * K], BF16, name="u_grouped", tag="u_grouped", align_bytes=64)
+            grouped = stage.tile([P, count * K], BF16, name="u_grouped", tag="u_grouped", align_bytes=256)
             u_grouped[first] = grouped
             turned = []
             for j in range(first, first + count):
-                pairs = u_raw[j].bitcast(F32)
+                elements = u_raw[j].bitcast(F32)
                 bank = next_bank()
                 for g in range(PASSES):
                     for h in range(2):
                         at = (2 * g + h) * P
                         nc.tensor.transpose(
-                            bank[:, at : at + P], pairs[:, 2 * P * g + h : 2 * P * (g + 1) : 2], identity[:]
+                            bank[:, at : at + P], elements[:, 2 * P * g + h : 2 * P * (g + 1) : 2], identity[:]
                         )
                 turned.append(bank)
-            for i in range(count):
-                copy = nc.scalar.copy if first + i in SCALAR_TURNED_ROWS else nc.vector.tensor_copy
-                side_by_side = grouped[:, i * K : (i + 1) * K].bitcast(F32)
+            for offset in range(count):
+                copy = nc.scalar.copy if first + offset in SCALAR_TURNED_ROWS else nc.vector.tensor_copy
+                side_by_side = grouped[:, offset * K : (offset + 1) * K].bitcast(F32)
                 copy(
                     out=side_by_side.rearrange("p (g r h) -> p g r h", g=PASSES, h=2),
-                    in_=turned[i][:].rearrange("p (g h r) -> p g r h", g=PASSES, h=2),
+                    in_=turned[offset][:].rearrange("p (g h r) -> p g r h", g=PASSES, h=2),
                 )
 
         def quantize_u(first, count):
@@ -178,14 +185,14 @@ def tile_sensing_residual_slope_s10_kernel(
         def interleave_d(g, n, half):
             if n not in d_grouped:
                 d_grouped[n] = stage.tile(
-                    [P, PASSES * N_TILE * PACK], BF16, name="d_grouped", tag="d_grouped", align_bytes=64
+                    [P, PASSES * N_TILE * PACK], BF16, name="d_grouped", tag="d_grouped", align_bytes=256
                 )
             width = N_TILE // 2
             at = (g * N_TILE + half * width) * PACK
-            first = n * N_TILE + half * width
+            left = n * N_TILE + half * width
             nc.scalar.copy(
                 out=d_grouped[n][:, at : at + width * PACK].rearrange("p (c t) -> p c t", t=PACK),
-                in_=d_raw[g][:, :, first : first + width].rearrange("p t c -> p c t"),
+                in_=d_raw[g][:, :, left : left + width].rearrange("p t c -> p c t"),
             )
 
         def quantize_d(n):
@@ -249,23 +256,23 @@ def tile_sensing_residual_slope_s10_kernel(
             store_residual(j, n)
 
         def slope_tile(j, n):
-            step = product(
+            change = product(
                 j,
                 [d_codes[:, cols(n * PASSES + g)].bitcast(FP8X4) for g in range(PASSES)],
                 [d_scales[:, cols(n * PASSES + g)] for g in range(PASSES)],
             )
             slope = stage.tile([P, N_TILE], F32, name="slope", tag="slope", bufs=16)
-            nc.vector.tensor_tensor(out=slope[:], in0=step[:], in1=residual[j][:, cols(n)], op=ALU.mult)
+            nc.vector.tensor_tensor(out=slope[:], in0=change[:], in1=residual[j][:, cols(n)], op=ALU.mult)
             nc.sync.dma_start(out=slope_rows[:, j, cols(n)], in_=slope[:])
 
-        steps = [(j, n) for j in range(2) for n in range(COL_TILES - 1)]
-        steps.extend([(j, COL_TILES - 1) for j in range(2)])
-        steps.extend([(j, n) for j in range(2, ROW_TILES) for n in range(COL_TILES)])
+        steps = [(j, n) for j in range(PAIR) for n in range(COL_TILES - 1)]
+        steps.extend([(j, COL_TILES - 1) for j in range(PAIR)])
+        steps.extend([(j, n) for j in range(PAIR, ROW_TILES) for n in range(COL_TILES)])
         slopes = [(j, n) for n in range(COL_TILES) for j in range(ROWS_BY_COLUMN)]
         slopes.extend([(j, n) for j in range(ROWS_BY_COLUMN, ROW_TILES) for n in range(COL_TILES)])
         halves = [(g, n, half) for g in range(PASSES) for n in range(COL_TILES - 1) for half in range(2)]
         halves.extend([(g, COL_TILES - 1, half) for g in range(PASSES) for half in range(2)])
-        turn_after = {steps.index((j, 0)) - TURN_AHEAD: j for j in range(2, ROW_TILES, 2)}
+        turn_after = {steps.index((j, 0)) - TURN_AHEAD: j for j in range(PAIR, ROW_TILES, PAIR)}
 
         turn_u(0, 1)
         quantize_u(0, 1)
@@ -282,9 +289,9 @@ def tile_sensing_residual_slope_s10_kernel(
             if i > 0:
                 finish(*steps[i - 1])
             if i - 1 in turn_after:
-                quantize_u(turn_after[i - 1], 2)
+                quantize_u(turn_after[i - 1], PAIR)
             for ready in range(COL_TILES):
-                if laid_out_at.get(ready) == i - 2:
+                if laid_out_at.get(ready) == i - D_QUANTIZE_LAG:
                     quantize_d(ready)
                     quantized_at[ready] = i
             if i >= FIRST_D_STEP and i != D_PAUSE_STEP:
@@ -294,7 +301,7 @@ def tile_sensing_residual_slope_s10_kernel(
                     if (g, half) == (PASSES - 1, 1):
                         laid_out_at[column] = i
             if i in turn_after:
-                turn_u(turn_after[i], 2)
+                turn_u(turn_after[i], PAIR)
             for row, column in slopes[:SLOPES_PER_STEP]:
                 if steps.index((row, column)) >= i or quantized_at.get(column, i) >= i:
                     break

from contextlib import ExitStack

import concourse.mybir as mybir
from concourse.masks import make_identity

M, K, N = 1024, 1024, 1536
FLOPS = 3 * 2 * M * K * N

F32 = mybir.dt.float32
BF16 = mybir.dt.bfloat16
I32 = mybir.dt.int32
U32 = mybir.dt.uint32
U8 = mybir.dt.uint8
FP8X4 = mybir.dt.float8_e4m3fn_x4
FP4X4 = mybir.dt.float4_e2m1fn_x4
ALU = mybir.AluOpType
SIGMOID = mybir.ActivationFunctionType.Sigmoid

P = 128
PACK = 4
PASSES = K // (P * PACK)
ROW_TILES = M // P
N_TILE = 512
COL_TILES = N // N_TILE
BANKS = 8
QUADRANT = 32
SCALE_ROWS = 4
QUADRANT_ORDER = (0, 2, 1, 3)
FP4_WORD_BYTES = 2
FP8_WORD_BYTES = 4
PAIR = 2

FIRST_GPSIMD_ROW = 4
SCALAR_TURNED_ROWS = range(1, 2 * PAIR)
TURN_AHEAD = 4
FIRST_D_STEP = 5
D_PAUSE_STEP = 9
D_QUANTIZE_LAG = 2
SLOPES_PER_STEP = 3
ROWS_BY_COLUMN = 6


def tile_sensing_residual_slope_s10_kernel(
    tc, u, v_words, v_scales, c_words, c_scales, d, y, out_0, out_1
):
    nc = tc.nc
    u_rows = u.rearrange("(p j) k -> p j k", j=ROW_TILES)
    y_rows = y.rearrange("(p j) n -> p j n", j=ROW_TILES)
    residual_rows = out_0.rearrange("(p j) n -> p j n", j=ROW_TILES)
    slope_rows = out_1.rearrange("(p j) n -> p j n", j=ROW_TILES)
    v_bytes = v_words.rearrange("g p x -> p g x")
    c_bytes = c_words.rearrange("g p n t -> p g (n t)")
    d_passes = d.rearrange("(g p t) n -> g p t n", g=PASSES, t=PACK)

    with ExitStack() as ctx:
        keep = ctx.enter_context(tc.tile_pool(name="keep", bufs=1))
        stage = ctx.enter_context(tc.tile_pool(name="stage", bufs=2))
        psum = ctx.enter_context(tc.psum_pool(name="psum", bufs=1))
        ctx.enter_context(tc.manual_schedule())

        banks_taken = []

        def next_bank():
            name = "bank%d" % (len(banks_taken) % BANKS)
            banks_taken.append(name)
            return psum.tile([P, N_TILE], F32, name=name, tag=name)

        def cols(n):
            return slice(n * N_TILE, (n + 1) * N_TILE)

        v_scale_tile = keep.tile([P, PASSES * N], U8, align_bytes=256)
        nc.vector.memset(v_scale_tile[:].bitcast(I32), 0)
        c_scale_tile = keep.tile([P, N], U8, align_bytes=256)
        nc.vector.memset(c_scale_tile[:].bitcast(I32), 0)
        identity = keep.tile([P, P], F32)
        make_identity(nc, identity[:])

        u_raw, y_raw, v_codes, c_codes, d_raw = {}, {}, {}, {}, {}

        def load_rows(loaded, hbm, name, first, count):
            width = hbm.shape[2]
            raw = keep.tile([P, count * width], BF16, name="%s%d" % (name, first), align_bytes=256)
            nc.sync.dma_start(
                out=raw[:].rearrange("p (j w) -> p j w", j=count), in_=hbm[:, first : first + count, :]
            )
            for offset in range(count):
                loaded[first + offset] = raw[:, offset * width : (offset + 1) * width]

        def load_u(first, count):
            load_rows(u_raw, u_rows, "u_raw", first, count)

        def load_y(first, count):
            load_rows(y_raw, y_rows, "y_raw", first, count)

        def load_words(loaded, hbm, name, word_bytes, first, count):
            width = N_TILE * word_bytes
            raw = keep.tile([P, PASSES * count * width], U8, name="%s%d" % (name, first), align_bytes=256)
            nc.sync.dma_start(
                out=raw[:].bitcast(I32).rearrange("p (g x) -> p g x", g=PASSES),
                in_=hbm[:, :, first * width : (first + count) * width].bitcast(I32),
            )
            for g in range(PASSES):
                for offset in range(count):
                    at = (g * count + offset) * width
                    loaded[(g, first + offset)] = raw[:, at : at + width]

        def load_v(first, count):
            load_words(v_codes, v_bytes, "v_codes", FP4_WORD_BYTES, first, count)

        def load_c(first, count):
            load_words(c_codes, c_bytes, "c_codes", FP8_WORD_BYTES, first, count)

        def load_d(g):
            raw = keep.tile([P, PACK, N], BF16, name="d_raw%d" % g, align_bytes=256)
            nc.sync.dma_start(out=raw[:], in_=d_passes[g])
            d_raw[g] = raw

        load_u(0, 1)
        for quadrant in QUADRANT_ORDER:
            top = QUADRANT * quadrant
            blocks = slice(SCALE_ROWS * quadrant, SCALE_ROWS * (quadrant + 1))
            nc.sync.dma_start(
                out=v_scale_tile[top : top + SCALE_ROWS, :].bitcast(I32).rearrange("r (g x) -> r g x", g=PASSES),
                in_=v_scales[:, blocks, :].rearrange("g r n -> r g n").bitcast(I32),
            )
        load_v(0, 1)
        for quadrant in QUADRANT_ORDER:
            top = QUADRANT * quadrant
            blocks = slice(SCALE_ROWS * quadrant, SCALE_ROWS * (quadrant + 1))
            nc.sync.dma_start(
                out=c_scale_tile[top + SCALE_ROWS : top + (PASSES + 1) * SCALE_ROWS, :].bitcast(I32),
                in_=c_scales[:, blocks, :].bitcast(I32),
            )
        load_c(0, 1)
        load_u(1, 1)
        load_v(1, COL_TILES - 1)
        load_c(1, 1)
        load_y(0, 1)
        load_u(2, PAIR)
        load_y(1, 1)
        load_c(2, 1)
        load_d(0)
        load_y(2, 1)
        load_u(4, PAIR)
        load_y(3, 1)
        load_d(1)
        load_y(4, PAIR)
        load_u(6, PAIR)
        load_y(6, PAIR)

        u_codes = keep.tile([P, ROW_TILES * PASSES * P], U32, align_bytes=256)
        u_scales = keep.tile([P, ROW_TILES * PASSES * P], U8, align_bytes=256)
        d_codes = keep.tile([P, COL_TILES * PASSES * N_TILE], U32, align_bytes=256)
        d_scales = keep.tile([P, COL_TILES * PASSES * N_TILE], U8, align_bytes=256)
        u_grouped, d_grouped = {}, {}

        def turn_u(first, count):
            grouped = stage.tile([P, count * K], BF16, name="u_grouped", tag="u_grouped", align_bytes=256)
            u_grouped[first] = grouped
            turned = []
            for j in range(first, first + count):
                elements = u_raw[j].bitcast(F32)
                bank = next_bank()
                for g in range(PASSES):
                    for h in range(2):
                        at = (2 * g + h) * P
                        nc.tensor.transpose(
                            bank[:, at : at + P], elements[:, 2 * P * g + h : 2 * P * (g + 1) : 2], identity[:]
                        )
                turned.append(bank)
            for offset in range(count):
                copy = nc.scalar.copy if first + offset in SCALAR_TURNED_ROWS else nc.vector.tensor_copy
                side_by_side = grouped[:, offset * K : (offset + 1) * K].bitcast(F32)
                copy(
                    out=side_by_side.rearrange("p (g r h) -> p g r h", g=PASSES, h=2),
                    in_=turned[offset][:].rearrange("p (g h r) -> p g r h", g=PASSES, h=2),
                )

        def quantize_u(first, count):
            at = slice(first * PASSES * P, (first + count) * PASSES * P)
            nc.vector.quantize_mx(
                out=u_codes[:, at].bitcast(FP8X4), scales=u_scales[:, at], in_=u_grouped[first][:]
            )

        def interleave_d(g, n, half):
            if n not in d_grouped:
                d_grouped[n] = stage.tile(
                    [P, PASSES * N_TILE * PACK], BF16, name="d_grouped", tag="d_grouped", align_bytes=256
                )
            width = N_TILE // 2
            at = (g * N_TILE + half * width) * PACK
            left = n * N_TILE + half * width
            nc.scalar.copy(
                out=d_grouped[n][:, at : at + width * PACK].rearrange("p (c t) -> p c t", t=PACK),
                in_=d_raw[g][:, :, left : left + width].rearrange("p t c -> p c t"),
            )

        def quantize_d(n):
            at = slice(n * PASSES * N_TILE, (n + 1) * PASSES * N_TILE)
            nc.vector.quantize_mx(out=d_codes[:, at].bitcast(FP8X4), scales=d_scales[:, at], in_=d_grouped[n][:])

        def product(j, moving, moving_scales):
            bank = next_bank()
            for g in range(PASSES):
                at = slice((j * PASSES + g) * P, (j * PASSES + g + 1) * P)
                nc.tensor.matmul_mx(
                    out=bank[:],
                    lhsT=u_codes[:, at].bitcast(FP8X4),
                    lhsT_scale=u_scales[:, at],
                    rhs=moving[g],
                    rhs_scale=moving_scales[g],
                    start=(g == 0),
                    stop=(g == PASSES - 1),
                )
            return bank

        residual, pred, weight = {}, {}, {}

        def predict(j, n):
            pred[(j, n)] = product(
                j,
                [v_codes[(g, n)].bitcast(FP4X4) for g in range(PASSES)],
                [v_scale_tile[:, cols(g * COL_TILES + n)] for g in range(PASSES)],
            )
            conf = product(
                j,
                [c_codes[(g, n)].bitcast(FP8X4) for g in range(PASSES)],
                [c_scale_tile[SCALE_ROWS * (g + 1) : P, cols(n)] for g in range(PASSES)],
            )
            weight[(j, n)] = stage.tile([P, N_TILE], F32, name="weight", tag="weight", bufs=8)
            nc.scalar.activation(out=weight[(j, n)][:], in_=conf[:], func=SIGMOID)

        def subtract(j, n):
            if n == 0:
                residual[j] = keep.tile([P, N], F32, name="residual%d" % j)
            nc.vector.tensor_tensor(
                out=residual[j][:, cols(n)], in0=pred[(j, n)][:], in1=y_raw[j][:, cols(n)], op=ALU.subtract
            )

        def weigh(engine, j, n):
            part = residual[j][:, cols(n)]
            engine.tensor_tensor(out=part, in0=part, in1=weight[(j, n)][:], op=ALU.mult)

        def store_residual(j, n):
            if j == ROW_TILES - 1:
                nc.sync.dma_start(out=residual_rows[:, j, cols(n)], in_=residual[j][:, cols(n)])
            elif n == COL_TILES - 1:
                nc.sync.dma_start(out=residual_rows[:, j, :], in_=residual[j][:])

        def on_gpsimd(j, n):
            return j >= FIRST_GPSIMD_ROW and (j, n) != (ROW_TILES - 1, COL_TILES - 1)

        def finish(j, n):
            if not on_gpsimd(j, n):
                weigh(nc.vector, j, n)
            store_residual(j, n)

        def slope_tile(j, n):
            change = product(
                j,
                [d_codes[:, cols(n * PASSES + g)].bitcast(FP8X4) for g in range(PASSES)],
                [d_scales[:, cols(n * PASSES + g)] for g in range(PASSES)],
            )
            slope = stage.tile([P, N_TILE], F32, name="slope", tag="slope", bufs=16)
            nc.vector.tensor_tensor(out=slope[:], in0=change[:], in1=residual[j][:, cols(n)], op=ALU.mult)
            nc.sync.dma_start(out=slope_rows[:, j, cols(n)], in_=slope[:])

        steps = [(j, n) for j in range(PAIR) for n in range(COL_TILES - 1)]
        steps.extend([(j, COL_TILES - 1) for j in range(PAIR)])
        steps.extend([(j, n) for j in range(PAIR, ROW_TILES) for n in range(COL_TILES)])
        slopes = [(j, n) for n in range(COL_TILES) for j in range(ROWS_BY_COLUMN)]
        slopes.extend([(j, n) for j in range(ROWS_BY_COLUMN, ROW_TILES) for n in range(COL_TILES)])
        halves = [(g, n, half) for g in range(PASSES) for n in range(COL_TILES - 1) for half in range(2)]
        halves.extend([(g, COL_TILES - 1, half) for g in range(PASSES) for half in range(2)])
        turn_after = {steps.index((j, 0)) - TURN_AHEAD: j for j in range(PAIR, ROW_TILES, PAIR)}

        turn_u(0, 1)
        quantize_u(0, 1)
        laid_out_at = {}
        quantized_at = {}
        for i, (j, n) in enumerate(steps):
            predict(j, n)
            if i == 0:
                turn_u(1, 1)
                quantize_u(1, 1)
            subtract(j, n)
            if on_gpsimd(j, n):
                weigh(nc.gpsimd, j, n)
            if i > 0:
                finish(*steps[i - 1])
            if i - 1 in turn_after:
                quantize_u(turn_after[i - 1], PAIR)
            for ready in range(COL_TILES):
                if laid_out_at.get(ready) == i - D_QUANTIZE_LAG:
                    quantize_d(ready)
                    quantized_at[ready] = i
            if i >= FIRST_D_STEP and i != D_PAUSE_STEP:
                for g, column, half in halves[: 2 if quantized_at.get(0, i) < i else 1]:
                    interleave_d(g, column, half)
                    halves.remove((g, column, half))
                    if (g, half) == (PASSES - 1, 1):
                        laid_out_at[column] = i
            if i in turn_after:
                turn_u(turn_after[i], PAIR)
            for row, column in slopes[:SLOPES_PER_STEP]:
                if steps.index((row, column)) >= i or quantized_at.get(column, i) >= i:
                    break
                slope_tile(row, column)
                slopes.remove((row, column))
        finish(*steps[-1])
        for row, column in slopes:
            slope_tile(row, column)
